import numpy as np
import ml_dtypes


def mxq(x, axis, fmt="e4m3"):
    dtype, down = {"e4m3": (ml_dtypes.float8_e4m3fn, 7), "e5m2": (ml_dtypes.float8_e5m2, 14)}[fmt]
    v = np.moveaxis(np.asarray(x, np.float32).astype(ml_dtypes.bfloat16).astype(np.float64), axis, -1)
    blocks = v.reshape(v.shape[:-1] + (-1, 32))
    amax = np.abs(blocks).max(-1, keepdims=True)
    byte = np.maximum(np.where(amax > 0, np.frexp(amax)[1] - 1 + 127, 0) - down, 1)
    scale = np.exp2(byte - 127.0)
    codes = (blocks / scale).astype(np.float32).astype(dtype).astype(np.float64)
    return np.moveaxis((codes * scale).reshape(v.shape), -1, axis)


WIDE = False


def mx_kscale(k):
    if not WIDE:
        return np.ones(k)
    levels = np.array([10, -10, 5, -5, 0])
    if k % 512:
        return np.exp2(np.random.permutation(np.resize(levels, k // 32))).repeat(32)
    a = np.empty((k // 512, 16))
    for p in range(k // 512):
        a[p, :8] = np.random.permutation(np.resize(levels, 8))
        for g in range(8):
            far = levels[np.abs(levels - a[p, g]) >= 10]
            a[p, g + 8] = far[np.random.randint(len(far))]
    return np.exp2(a.ravel()).repeat(32)


def f64(x):
    return np.asarray(x).astype(np.float64)


def striped(idx):
    return np.tile(idx.reshape(-1, 16).T, (8, 1)).astype(np.uint16)


def unstriped(offs):
    return offs[:16].T.reshape(-1).astype(np.int64)


E2M1 = np.array([0.0, 0.5, 1.0, 1.5, 2.0, 3.0, 4.0, 6.0, -0.0, -0.5, -1.0, -1.5, -2.0, -3.0, -4.0, -6.0])


def pack_weight(w, fmt):
    k, n = w.shape
    w = f64(np.asarray(w, np.float32).astype(ml_dtypes.bfloat16)).reshape(k // 32, 32, n)
    amax = np.abs(w).max(1)
    if fmt == "e4m3":
        byte = np.frexp(amax)[1] - 1 + 127 - 7
    else:
        mant, ex = np.frexp(amax / 6.0)
        byte = np.where(mant > 0.5, ex, ex - 1) + 127
    byte = np.clip(np.where(amax > 0, byte, 1), 1, 254)
    scaled = (w * np.exp2(127.0 - byte)[:, None, :]).reshape(k, n).astype(np.float32)
    by_word = np.ascontiguousarray(scaled.reshape(k // 512, 128, 4, n).transpose(0, 1, 3, 2))
    if fmt == "e4m3":
        words = by_word.astype(ml_dtypes.float8_e4m3fn).view(np.uint8)
    else:
        c = by_word.astype(ml_dtypes.float4_e2m1fn).view(np.uint8) & 0xF
        words = (c[..., 0::2] | (c[..., 1::2] << 4)).reshape(k // 512, 128, 2 * n)
    return np.ascontiguousarray(words), np.ascontiguousarray(byte.astype(np.uint8).reshape(k // 512, 16, n))


def unpack_weight(words, scales, fmt):
    g, _, n = scales.shape
    words = np.ascontiguousarray(words).reshape(g, 128, n, -1)
    if fmt == "e4m3":
        vals = words.view(ml_dtypes.float8_e4m3fn).astype(np.float64)
    else:
        nib = np.empty((g, 128, n, 4), np.uint8)
        nib[..., 0::2] = words & 0xF
        nib[..., 1::2] = words >> 4
        vals = E2M1[nib]
    vals = vals * np.repeat(np.exp2(scales.astype(np.float64) - 127.0), 8, axis=1)[..., None]
    return vals.transpose(0, 1, 3, 2).reshape(g * 512, n)


def gelu(v):
    return 0.5 * v * (1.0 + np.tanh(np.sqrt(2.0 / np.pi) * (v + 0.044715 * v**3)))


K, T, E, C, H, N = 1024, 640, 6, 128, 512, 128
TOP = 3
PAD = 64


def by_expert(wq, xq):
    return np.concatenate([wq[e].T @ xq[:, e * C:(e + 1) * C] for e in range(E)], axis=1)


def setup_inputs():
    n = np.random.standard_normal
    s = mx_kscale(K)[:, None]
    u = mx_kscale(H)
    slot_token = np.empty(E * C, np.int64); pos = np.tile(E * C + np.arange(T) % PAD, (TOP, 1)); taken = np.zeros(T, np.int64)
    liked = np.random.randn(T)
    for e in np.random.permutation(E):
        free = np.flatnonzero(taken < TOP); pick = np.random.permutation(free[np.argsort(-(liked[free] + np.random.gumbel(size=free.size)))[:C]]); slot_token[e * C:(e + 1) * C] = pick
        pos[taken[pick], pick] = e * C + np.arange(C); taken[pick] += 1
    g = np.random.uniform(0.2, 0.8, (TOP, T))
    w1 = [pack_weight(m, "e2m1") for m in n((E, K, H)) / np.sqrt(K) / s[None]]
    w3 = [pack_weight(m, "e2m1") for m in n((E, K, H)) / np.sqrt(K) / s[None] * u[None, None, :]]
    w2 = [pack_weight(m, "e2m1") for m in n((E, H, N)) / np.sqrt(H) / u[None, :, None]]
    return {
        "xT": (n((K, T)) * s).astype(np.float32),
        "w1_words": np.stack([m[0] for m in w1]),
        "w1_scales": np.stack([m[1] for m in w1]),
        "w3_words": np.stack([m[0] for m in w3]),
        "w3_scales": np.stack([m[1] for m in w3]),
        "w2_words": np.stack([m[0] for m in w2]),
        "w2_scales": np.stack([m[1] for m in w2]),
        "gate": np.stack([np.tile(r, (N, 1)) for r in g]).astype(np.float32),
        "offs": striped(slot_token),
        "pos1": striped(pos[0]),
        "pos2": striped(pos[1]),
        "pos3": striped(pos[2]),
    }


def reference(xT, w1_words, w1_scales, w3_words, w3_scales, w2_words, w2_scales, gate, offs, pos1, pos2, pos3):
    idx = unstriped(offs)
    w1 = np.stack([unpack_weight(w1_words[e], w1_scales[e], "e2m1") for e in range(E)])
    w3 = np.stack([unpack_weight(w3_words[e], w3_scales[e], "e2m1") for e in range(E)])
    w2 = np.stack([unpack_weight(w2_words[e], w2_scales[e], "e2m1") for e in range(E)])
    xq = mxq(f64(xT)[:, idx], 0, "e4m3")
    h = gelu(by_expert(w1, xq))
    h = h * by_expert(w3, xq)
    y = by_expert(w2, mxq(h, 0, "e4m3"))
    y = np.concatenate([y, np.zeros((N, PAD))], axis=1)
    return sum(f64(gate[r]) * y[:, unstriped(p)] for r, p in enumerate((pos1, pos2, pos3)))

@@ -1,0 +1,226 @@
+from contextlib import ExitStack
+
+import concourse.mybir as mybir
+from concourse.masks import make_identity
+
+K, T, E, C, H, N = 1024, 640, 6, 128, 512, 128
+TOP = 3
+PAD = 64
+SLOTS = E * C
+FLOPS = 2 * SLOTS * (2 * K * H + H * N)
+
+F32 = mybir.dt.float32
+BF16 = mybir.dt.bfloat16
+I32 = mybir.dt.int32
+U32 = mybir.dt.uint32
+U16 = mybir.dt.uint16
+U8 = mybir.dt.uint8
+FP8X4 = mybir.dt.float8_e4m3fn_x4
+FP4X4 = mybir.dt.float4_e2m1fn_x4
+ACT = mybir.ActivationFunctionType
+MULT = mybir.AluOpType.mult
+ADD = mybir.AluOpType.add
+
+P = 128
+PACK = 4
+K_PASS = P * PACK
+PASSES = K // K_PASS
+LIST = 16
+GROUP = 3
+AHEAD = 3
+
+LOADS = ((0, 512), (512, 128))
+CASTS = (
+    ((0, 256, "vector"), (256, 128, "vector"), (384, 128, "scalar"), (512, 128, "scalar")),
+    ((0, 256, "scalar"), (256, 256, "vector"), (512, 128, "scalar")),
+)
+BANKS_OF_Y = ((0, 1, 2, 3), (4,), (5,))
+OUT_PARTS = ((0, 256), (256, 256), (512, 128))
+
+
+def tile_moe_ecr_glu_gelu_kernel(
+    tc, xT, w1_words, w1_scales, w3_words, w3_scales, w2_words, w2_scales, gate, offs, pos1, pos2, pos3, out
+):
+    nc = tc.nc
+
+    with ExitStack() as ctx:
+        lists = ctx.enter_context(tc.tile_pool(name="lists", bufs=1))
+        keep = ctx.enter_context(tc.tile_pool(name="keep", bufs=1))
+        work = ctx.enter_context(tc.tile_pool(name="work", bufs=4))
+        ring = ctx.enter_context(tc.tile_pool(name="ring", bufs=AHEAD))
+        psum = ctx.enter_context(tc.psum_pool(name="psum", bufs=2))
+
+        def held(name, shape, dtype):
+            return keep.tile(shape, dtype, name=name, align_bytes=64)
+
+        def load_scale_rows(plane, scales):
+            rows = scales.rearrange("e s (q r) n -> r q (e s) n", r=4).bitcast(I32)
+            words = plane[:].bitcast(I32).rearrange("p (a n) -> p a n", n=rows.shape[3])
+            for r in range(4):
+                nc.sync.dma_start(out=words[r:P:32], in_=rows[r])
+
+        groups = E // GROUP
+        w_planes = [[held(f"w{m}_plane{g}", [P, GROUP * PASSES * H], U8) for m in range(2)] for g in range(groups)]
+        w2_plane = held("w2_plane", [P, E * N], U8)
+        for plane in w_planes[0] + w_planes[1] + [w2_plane]:
+            nc.vector.memset(plane[:].bitcast(I32), 0)
+        x_planes = [held(f"x_plane{s}", [P, T], U8) for s in range(PASSES)]
+        x_codes = [held(f"x_codes{s}", [P, T], U32) for s in range(PASSES)]
+        zeros = held("zeros", [P, PAD], F32)
+        nc.gpsimd.memset(zeros[:], 0.0)
+        for plane in x_planes:
+            nc.gpsimd.memset(plane[:], 0)
+        ident = held("ident", [P, P], F32)
+        make_identity(nc, ident[:])
+        y = held("y", [P, SLOTS + PAD], F32)
+        nc.scalar.activation(out=y[:, SLOTS:], in_=zeros[:], func=ACT.Gelu_apprx_tanh)
+
+        offs_sb = lists.tile([P, SLOTS // LIST], U16, name="offs_sb")
+        raw = {}
+        for s in range(PASSES):
+            rows = xT[s * K_PASS:(s + 1) * K_PASS, :].rearrange("(p j) t -> p j t", j=PACK)
+            for t0, width in LOADS:
+                raw[s, t0] = held(f"raw{s}_{t0}", [P, PACK, width], F32)
+                nc.sync.dma_start(out=raw[s, t0][:], in_=rows[:, :, t0:t0 + width])
+            if s == 0:
+                nc.sync.dma_start(offs_sb[:], offs)
+
+        w_words = {}
+        w2_sb = held("w2_sb", [P, E * 2 * N], U8)
+        for e in range(E):
+            g = e // GROUP
+            if e % GROUP == 0:
+                for m, scales in enumerate((w1_scales, w3_scales)):
+                    load_scale_rows(w_planes[g][m], scales[g * GROUP:(g + 1) * GROUP])
+            for m, words in enumerate((w1_words, w3_words)):
+                w_words[e, m] = held(f"w{m}_words{e}", [P, PASSES * 2 * H], U8)
+                nc.sync.dma_start(
+                    out=w_words[e, m][:].bitcast(I32).rearrange("p (s b) -> p s b", s=PASSES),
+                    in_=words[e].rearrange("s p b -> p s b").bitcast(I32),
+                )
+        load_scale_rows(w2_plane, w2_scales)
+        nc.sync.dma_start(
+            out=w2_sb[:].bitcast(I32).rearrange("p (e b) -> p e b", e=E),
+            in_=w2_words.rearrange("e s p b -> p (e s) b").bitcast(I32),
+        )
+        pos_sb = []
+        for r, pos in enumerate((pos1, pos2, pos3)):
+            pos_sb.append(lists.tile([P, T // LIST], U16, name=f"pos_sb{r}"))
+            nc.sync.dma_start(pos_sb[r][:], pos)
+        gate_sb = {}
+        for t0, width in OUT_PARTS:
+            gate_sb[t0] = held(f"gate{t0}", [P, TOP * width], F32)
+            nc.sync.dma_start(
+                out=gate_sb[t0][:].rearrange("n (r t) -> n r t", r=TOP),
+                in_=gate[:, :, t0:t0 + width].rearrange("r n t -> n r t"),
+            )
+
+        slot_codes, slot_planes = {}, {}
+
+        def quantise_tokens(s):
+            for t0, width, engine in CASTS[s]:
+                l0 = max(first for first, count in LOADS if first <= t0)
+                src = raw[s, l0][:, :, t0 - l0:t0 - l0 + width].rearrange("p j (c i) -> p c j i", i=4)
+                grouped = held(f"grouped{s}_{t0}", [P, width * PACK], BF16)
+                dst = grouped[:].rearrange("p (c i j) -> p c j i", i=4, j=PACK)
+                if engine == "vector":
+                    nc.vector.tensor_copy(out=dst, in_=src)
+                else:
+                    nc.scalar.activation(out=dst, in_=src, func=ACT.Copy)
+                nc.vector.quantize_mx(
+                    out=x_codes[s][:, t0:t0 + width].bitcast(FP8X4),
+                    scales=x_planes[s][:, t0:t0 + width],
+                    in_=grouped[:],
+                )
+
+        def gather_tokens(s, e):
+            cols = C // LIST
+            part = offs_sb[:, e * cols:(e + 1) * cols]
+            slot_codes[s, e] = ring.tile([P, C], U32, name=f"slot_codes{s}", align_bytes=64)
+            slot_planes[s, e] = ring.tile([P, C], U8, name=f"slot_plane{s}", align_bytes=64)
+            nc.vector.tensor_copy(slot_codes[s, e][:], x_codes[s][:].indirect(part))
+            nc.vector.tensor_copy(slot_planes[s, e][:], x_planes[s][:].indirect(part))
+
+        for s in range(PASSES):
+            quantise_tokens(s)
+            for e in range(AHEAD):
+                gather_tokens(s, e)
+
+        hidden, h_codes, h_plane = {}, {}, {}
+
+        def first_layer(e):
+            g = e // GROUP
+            sums = []
+            for m in range(2):
+                acc = psum.tile([P, H], F32, name=f"acc{m}", bufs=3)
+                for s in range(PASSES):
+                    first = ((e % GROUP) * PASSES + s) * H
+                    nc.tensor.matmul_mx(
+                        out=acc[:],
+                        lhsT=slot_codes[s, e][:].bitcast(FP8X4),
+                        lhsT_scale=slot_planes[s, e][:],
+                        rhs=w_words[e, m][:, s * 2 * H:(s + 1) * 2 * H].bitcast(FP4X4),
+                        rhs_scale=w_planes[g][m][:, first:first + H],
+                        start=(s == 0),
+                        stop=(s == PASSES - 1),
+                    )
+                sums.append(acc[:].rearrange("c (p u v) -> c u p v", u=2, v=2))
+            act = work.tile([P, H], F32, name="act")
+            act_view = act[:].rearrange("c (u p v) -> c u p v", u=2, v=2)
+            nc.scalar.activation(out=act_view, in_=sums[0], func=ACT.Gelu_apprx_tanh)
+            hidden[e] = work.tile([P, H], BF16, name="hidden")
+            nc.vector.tensor_tensor(
+                hidden[e][:].rearrange("c (u p v) -> c u p v", u=2, v=2), sums[1], act_view, MULT
+            )
+
+        def turn_hidden(e):
+            pairs = hidden[e][:].bitcast(F32)
+            turned = psum.tile([P, 2, C], F32, name="turned")
+            for u in range(2):
+                nc.tensor.transpose(turned[:, u, :], pairs[:, u * P:(u + 1) * P], ident[:])
+            grouped_h = work.tile([P, C * PACK], BF16, name="grouped_h", align_bytes=64)
+            nc.scalar.copy(
+                out=grouped_h[:].bitcast(F32).rearrange("p (c u) -> p c u", u=2),
+                in_=turned[:].rearrange("p u c -> p c u"),
+            )
+            h_codes[e] = held(f"h_codes{e}", [P, C], U32)
+            h_plane[e] = held(f"h_plane{e}", [P, C], U8)
+            nc.vector.quantize_mx(out=h_codes[e][:].bitcast(FP8X4), scales=h_plane[e][:], in_=grouped_h[:])
+
+        def second_layer(experts):
+            y_acc = psum.tile([P, len(experts) * C], F32, name="acc0", bufs=3)
+            for i, e in enumerate(experts):
+                nc.tensor.matmul_mx(
+                    out=y_acc[:, i * C:(i + 1) * C],
+                    lhsT=w2_sb[:, e * 2 * N:(e + 1) * 2 * N].bitcast(FP4X4),
+                    lhsT_scale=w2_plane[:, e * N:(e + 1) * N],
+                    rhs=h_codes[e][:].bitcast(FP8X4),
+                    rhs_scale=h_plane[e][:],
+                    start=True,
+                    stop=True,
+                )
+            nc.scalar.copy(out=y[:, experts[0] * C:(experts[-1] + 1) * C], in_=y_acc[:])
+
+        for step in range(E + 1):
+            if step < E:
+                first_layer(step)
+            if step >= 1:
+                turn_hidden(step - 1)
+            if step + AHEAD < E:
+                for s in range(PASSES):
+                    gather_tokens(s, step + AHEAD)
+        for experts in BANKS_OF_Y:
+            second_layer(experts)
+
+        for t0, width in OUT_PARTS:
+            terms = []
+            for r in range(TOP):
+                term = held(f"term{r}_{t0}", [P, width], F32)
+                part = pos_sb[r][:, t0 // LIST:(t0 + width) // LIST]
+                nc.vector.tensor_tensor(term[:], y[:].indirect(part), gate_sb[t0][:, r * width:(r + 1) * width], MULT)
+                terms.append(term)
+            partial = held(f"partial{t0}", [P, width], F32)
+            nc.vector.tensor_tensor(partial[:], terms[0][:], terms[1][:], ADD)
+            total = held(f"total{t0}", [P, width], F32)
+            nc.vector.tensor_tensor(total[:], partial[:], terms[2][:], ADD)
+            nc.sync.dma_start(out=out[:, t0:t0 + width], in_=total[:])

@@ -26,16 +26,18 @@ PACK = 4
 K_PASS = P * PACK
 PASSES = K // K_PASS
 LIST = 16
-GROUP = 3
-AHEAD = 3
+PAIR = 2
+PAIRS_HELD = 2
 
-LOADS = ((0, 512), (512, 128))
+LOADS = (((0, 256), (256, 256), (512, 128)), ((0, 256), (256, 384)))
 CASTS = (
-    ((0, 256, "vector"), (256, 128, "vector"), (384, 128, "scalar"), (512, 128, "scalar")),
-    ((0, 256, "scalar"), (256, 256, "vector"), (512, 128, "scalar")),
+    ((0, 128, "vector"), (128, 128, "scalar"), (256, 256, "scalar"), (512, 128, "vector")),
+    ((0, 256, "scalar"), (256, 256, "scalar"), (512, 128, "scalar")),
 )
+WEIGHT_LOADS = ((0, 1), (2, 3), (4,), (5,))
+LAG = 2
 BANKS_OF_Y = ((0, 1, 2, 3), (4,), (5,))
-OUT_PARTS = ((0, 256), (256, 256), (512, 128))
+OUT_PARTS = ((0, 512), (512, 128))
 
 
 def tile_moe_ecr_glu_gelu_kernel(
@@ -47,7 +49,7 @@ def tile_moe_ecr_glu_gelu_kernel(
         lists = ctx.enter_context(tc.tile_pool(name="lists", bufs=1))
         keep = ctx.enter_context(tc.tile_pool(name="keep", bufs=1))
         work = ctx.enter_context(tc.tile_pool(name="work", bufs=4))
-        ring = ctx.enter_context(tc.tile_pool(name="ring", bufs=AHEAD))
+        ring = ctx.enter_context(tc.tile_pool(name="ring", bufs=PAIRS_HELD))
         psum = ctx.enter_context(tc.psum_pool(name="psum", bufs=2))
 
         def held(name, shape, dtype):
@@ -59,17 +61,16 @@ def tile_moe_ecr_glu_gelu_kernel(
             for r in range(4):
                 nc.sync.dma_start(out=words[r:P:32], in_=rows[r])
 
-        groups = E // GROUP
-        w_planes = [[held(f"w{m}_plane{g}", [P, GROUP * PASSES * H], U8) for m in range(2)] for g in range(groups)]
+        w_planes = [held(f"w{m}_plane", [P, E * PASSES * H], U8) for m in range(2)]
         w2_plane = held("w2_plane", [P, E * N], U8)
-        for plane in w_planes[0] + w_planes[1] + [w2_plane]:
+        for plane in w_planes + [w2_plane]:
             nc.vector.memset(plane[:].bitcast(I32), 0)
         x_planes = [held(f"x_plane{s}", [P, T], U8) for s in range(PASSES)]
         x_codes = [held(f"x_codes{s}", [P, T], U32) for s in range(PASSES)]
         zeros = held("zeros", [P, PAD], F32)
         nc.gpsimd.memset(zeros[:], 0.0)
         for plane in x_planes:
-            nc.gpsimd.memset(plane[:], 0)
+            nc.gpsimd.memset(plane[:].bitcast(I32), 0)
         ident = held("ident", [P, P], F32)
         make_identity(nc, ident[:])
         y = held("y", [P, SLOTS + PAD], F32)
@@ -79,7 +80,7 @@ def tile_moe_ecr_glu_gelu_kernel(
         raw = {}
         for s in range(PASSES):
             rows = xT[s * K_PASS:(s + 1) * K_PASS, :].rearrange("(p j) t -> p j t", j=PACK)
-            for t0, width in LOADS:
+            for t0, width in LOADS[s]:
                 raw[s, t0] = held(f"raw{s}_{t0}", [P, PACK, width], F32)
                 nc.sync.dma_start(out=raw[s, t0][:], in_=rows[:, :, t0:t0 + width])
             if s == 0:
@@ -87,17 +88,17 @@ def tile_moe_ecr_glu_gelu_kernel(
 
         w_words = {}
         w2_sb = held("w2_sb", [P, E * 2 * N], U8)
-        for e in range(E):
-            g = e // GROUP
-            if e % GROUP == 0:
-                for m, scales in enumerate((w1_scales, w3_scales)):
-                    load_scale_rows(w_planes[g][m], scales[g * GROUP:(g + 1) * GROUP])
+        for m, scales in enumerate((w1_scales, w3_scales)):
+            load_scale_rows(w_planes[m], scales)
+        for experts in WEIGHT_LOADS:
             for m, words in enumerate((w1_words, w3_words)):
-                w_words[e, m] = held(f"w{m}_words{e}", [P, PASSES * 2 * H], U8)
+                block = held(f"w{m}_words{experts[0]}", [P, len(experts) * PASSES * 2 * H], U8)
                 nc.sync.dma_start(
-                    out=w_words[e, m][:].bitcast(I32).rearrange("p (s b) -> p s b", s=PASSES),
-                    in_=words[e].rearrange("s p b -> p s b").bitcast(I32),
+                    out=block[:].bitcast(I32).rearrange("p (a b) -> p a b", a=len(experts) * PASSES),
+                    in_=words[experts[0]:experts[-1] + 1].rearrange("e s p b -> p (e s) b").bitcast(I32),
                 )
+                for i, e in enumerate(experts):
+                    w_words[e, m] = block[:, i * PASSES * 2 * H:(i + 1) * PASSES * 2 * H]
         load_scale_rows(w2_plane, w2_scales)
         nc.sync.dma_start(
             out=w2_sb[:].bitcast(I32).rearrange("p (e b) -> p e b", e=E),
@@ -107,19 +108,15 @@ def tile_moe_ecr_glu_gelu_kernel(
         for r, pos in enumerate((pos1, pos2, pos3)):
             pos_sb.append(lists.tile([P, T // LIST], U16, name=f"pos_sb{r}"))
             nc.sync.dma_start(pos_sb[r][:], pos)
-        gate_sb = {}
-        for t0, width in OUT_PARTS:
-            gate_sb[t0] = held(f"gate{t0}", [P, TOP * width], F32)
-            nc.sync.dma_start(
-                out=gate_sb[t0][:].rearrange("n (r t) -> n r t", r=TOP),
-                in_=gate[:, :, t0:t0 + width].rearrange("r n t -> n r t"),
-            )
+        gate_sb = [held(f"gate{r}", [P, T], F32) for r in range(TOP)]
+        for r in range(TOP):
+            nc.sync.dma_start(out=gate_sb[r][:], in_=gate[r])
 
         slot_codes, slot_planes = {}, {}
 
         def quantise_tokens(s):
             for t0, width, engine in CASTS[s]:
-                l0 = max(first for first, count in LOADS if first <= t0)
+                l0 = max(first for first, count in LOADS[s] if first <= t0)
                 src = raw[s, l0][:, :, t0 - l0:t0 - l0 + width].rearrange("p j (c i) -> p c j i", i=4)
                 grouped = held(f"grouped{s}_{t0}", [P, width * PACK], BF16)
                 dst = grouped[:].rearrange("p (c i j) -> p c j i", i=4, j=PACK)
@@ -133,34 +130,33 @@ def tile_moe_ecr_glu_gelu_kernel(
                     in_=grouped[:],
                 )
 
-        def gather_tokens(s, e):
-            cols = C // LIST
-            part = offs_sb[:, e * cols:(e + 1) * cols]
-            slot_codes[s, e] = ring.tile([P, C], U32, name=f"slot_codes{s}", align_bytes=64)
-            slot_planes[s, e] = ring.tile([P, C], U8, name=f"slot_plane{s}", align_bytes=64)
-            nc.vector.tensor_copy(slot_codes[s, e][:], x_codes[s][:].indirect(part))
-            nc.vector.tensor_copy(slot_planes[s, e][:], x_planes[s][:].indirect(part))
+        def gather_tokens(s, pair):
+            part = offs_sb[:, pair * PAIR * C // LIST:(pair + 1) * PAIR * C // LIST]
+            slot_codes[s, pair] = ring.tile([P, PAIR * C], U32, name=f"slot_codes{s}", align_bytes=64)
+            slot_planes[s, pair] = ring.tile([P, PAIR * C], U8, name=f"slot_plane{s}", align_bytes=64)
+            nc.vector.tensor_copy(slot_codes[s, pair][:], x_codes[s][:].indirect(part))
+            nc.vector.tensor_copy(slot_planes[s, pair][:], x_planes[s][:].indirect(part))
 
         for s in range(PASSES):
             quantise_tokens(s)
-            for e in range(AHEAD):
-                gather_tokens(s, e)
+            for pair in range(PAIRS_HELD):
+                gather_tokens(s, pair)
 
         hidden, h_codes, h_plane = {}, {}, {}
 
         def first_layer(e):
-            g = e // GROUP
             sums = []
             for m in range(2):
                 acc = psum.tile([P, H], F32, name=f"acc{m}", bufs=3)
                 for s in range(PASSES):
-                    first = ((e % GROUP) * PASSES + s) * H
+                    first = (e * PASSES + s) * H
+                    slots = slice((e % PAIR) * C, (e % PAIR + 1) * C)
                     nc.tensor.matmul_mx(
                         out=acc[:],
-                        lhsT=slot_codes[s, e][:].bitcast(FP8X4),
-                        lhsT_scale=slot_planes[s, e][:],
+                        lhsT=slot_codes[s, e // PAIR][:, slots].bitcast(FP8X4),
+                        lhsT_scale=slot_planes[s, e // PAIR][:, slots],
                         rhs=w_words[e, m][:, s * 2 * H:(s + 1) * 2 * H].bitcast(FP4X4),
-                        rhs_scale=w_planes[g][m][:, first:first + H],
+                        rhs_scale=w_planes[m][:, first:first + H],
                         start=(s == 0),
                         stop=(s == PASSES - 1),
                     )
@@ -188,7 +184,7 @@ def tile_moe_ecr_glu_gelu_kernel(
             nc.vector.quantize_mx(out=h_codes[e][:].bitcast(FP8X4), scales=h_plane[e][:], in_=grouped_h[:])
 
         def second_layer(experts):
-            y_acc = psum.tile([P, len(experts) * C], F32, name="acc0", bufs=3)
+            y_acc = psum.tile([P, len(experts) * C], F32, name="acc1", bufs=3)
             for i, e in enumerate(experts):
                 nc.tensor.matmul_mx(
                     out=y_acc[:, i * C:(i + 1) * C],
@@ -201,14 +197,14 @@ def tile_moe_ecr_glu_gelu_kernel(
                 )
             nc.scalar.copy(out=y[:, experts[0] * C:(experts[-1] + 1) * C], in_=y_acc[:])
 
-        for step in range(E + 1):
+        for step in range(E + LAG):
             if step < E:
                 first_layer(step)
-            if step >= 1:
-                turn_hidden(step - 1)
-            if step + AHEAD < E:
+            if step == PAIR - 1:
                 for s in range(PASSES):
-                    gather_tokens(s, step + AHEAD)
+                    gather_tokens(s, PAIRS_HELD)
+            if step >= LAG:
+                turn_hidden(step - LAG)
         for experts in BANKS_OF_Y:
             second_layer(experts)
 
@@ -217,7 +213,7 @@ def tile_moe_ecr_glu_gelu_kernel(
             for r in range(TOP):
                 term = held(f"term{r}_{t0}", [P, width], F32)
                 part = pos_sb[r][:, t0 // LIST:(t0 + width) // LIST]
-                nc.vector.tensor_tensor(term[:], y[:].indirect(part), gate_sb[t0][:, r * width:(r + 1) * width], MULT)
+                nc.vector.tensor_tensor(term[:], y[:].indirect(part), gate_sb[r][:, t0:t0 + width], MULT)
                 terms.append(term)
             partial = held(f"partial{t0}", [P, width], F32)
             nc.vector.tensor_tensor(partial[:], terms[0][:], terms[1][:], ADD)

@@ -26,18 +26,17 @@ PACK = 4
 K_PASS = P * PACK
 PASSES = K // K_PASS
 LIST = 16
-PAIR = 2
-PAIRS_HELD = 2
+AHEAD = 3
 
-LOADS = (((0, 256), (256, 256), (512, 128)), ((0, 256), (256, 384)))
 CASTS = (
-    ((0, 128, "vector"), (128, 128, "scalar"), (256, 256, "scalar"), (512, 128, "vector")),
-    ((0, 256, "scalar"), (256, 256, "scalar"), (512, 128, "scalar")),
+    ((0, 256, "vector"), (256, 256, "scalar"), (512, 128, "vector")),
+    ((0, 256, "scalar"), (256, 256, "scalar"), (512, 128, "vector")),
 )
-WEIGHT_LOADS = ((0, 1), (2, 3), (4,), (5,))
+SCALE_GROUPS = ((0, 1, 2), (3, 4, 5))
 LAG = 2
 BANKS_OF_Y = ((0, 1, 2, 3), (4,), (5,))
-OUT_PARTS = ((0, 512), (512, 128))
+HEAD = 256
+BANKS = (2, 4)
 
 
 def tile_moe_ecr_glu_gelu_kernel(
@@ -49,7 +48,7 @@ def tile_moe_ecr_glu_gelu_kernel(
         lists = ctx.enter_context(tc.tile_pool(name="lists", bufs=1))
         keep = ctx.enter_context(tc.tile_pool(name="keep", bufs=1))
         work = ctx.enter_context(tc.tile_pool(name="work", bufs=4))
-        ring = ctx.enter_context(tc.tile_pool(name="ring", bufs=PAIRS_HELD))
+        ring = ctx.enter_context(tc.tile_pool(name="ring", bufs=AHEAD))
         psum = ctx.enter_context(tc.psum_pool(name="psum", bufs=2))
 
         def held(name, shape, dtype):
@@ -61,9 +60,12 @@ def tile_moe_ecr_glu_gelu_kernel(
             for r in range(4):
                 nc.sync.dma_start(out=words[r:P:32], in_=rows[r])
 
-        w_planes = [held(f"w{m}_plane", [P, E * PASSES * H], U8) for m in range(2)]
+        w_planes = [
+            [held(f"w{m}_plane{g}", [P, len(experts) * PASSES * H], U8) for m in range(2)]
+            for g, experts in enumerate(SCALE_GROUPS)
+        ]
         w2_plane = held("w2_plane", [P, E * N], U8)
-        for plane in w_planes + [w2_plane]:
+        for plane in w_planes[0] + w_planes[1] + [w2_plane]:
             nc.vector.memset(plane[:].bitcast(I32), 0)
         x_planes = [held(f"x_plane{s}", [P, T], U8) for s in range(PASSES)]
         x_codes = [held(f"x_codes{s}", [P, T], U32) for s in range(PASSES)]
@@ -80,25 +82,25 @@ def tile_moe_ecr_glu_gelu_kernel(
         raw = {}
         for s in range(PASSES):
             rows = xT[s * K_PASS:(s + 1) * K_PASS, :].rearrange("(p j) t -> p j t", j=PACK)
-            for t0, width in LOADS[s]:
-                raw[s, t0] = held(f"raw{s}_{t0}", [P, PACK, width], F32)
-                nc.sync.dma_start(out=raw[s, t0][:], in_=rows[:, :, t0:t0 + width])
+            raw[s] = held(f"raw{s}", [P, PACK, T], F32)
+            nc.sync.dma_start(out=raw[s][:], in_=rows)
             if s == 0:
                 nc.sync.dma_start(offs_sb[:], offs)
 
         w_words = {}
         w2_sb = held("w2_sb", [P, E * 2 * N], U8)
-        for m, scales in enumerate((w1_scales, w3_scales)):
-            load_scale_rows(w_planes[m], scales)
-        for experts in WEIGHT_LOADS:
-            for m, words in enumerate((w1_words, w3_words)):
-                block = held(f"w{m}_words{experts[0]}", [P, len(experts) * PASSES * 2 * H], U8)
-                nc.sync.dma_start(
-                    out=block[:].bitcast(I32).rearrange("p (a b) -> p a b", a=len(experts) * PASSES),
-                    in_=words[experts[0]:experts[-1] + 1].rearrange("e s p b -> p (e s) b").bitcast(I32),
-                )
-                for i, e in enumerate(experts):
-                    w_words[e, m] = block[:, i * PASSES * 2 * H:(i + 1) * PASSES * 2 * H]
+        w_plane = {}
+        for g, experts in enumerate(SCALE_GROUPS):
+            for m, scales in enumerate((w1_scales, w3_scales)):
+                load_scale_rows(w_planes[g][m], scales[experts[0]:experts[-1] + 1])
+            for i, e in enumerate(experts):
+                for m, words in enumerate((w1_words, w3_words)):
+                    w_plane[e, m] = w_planes[g][m][:, i * PASSES * H:(i + 1) * PASSES * H]
+                    w_words[e, m] = held(f"w{m}_words{e}", [P, PASSES * 2 * H], U8)
+                    nc.sync.dma_start(
+                        out=w_words[e, m][:].bitcast(I32).rearrange("p (s b) -> p s b", s=PASSES),
+                        in_=words[e].rearrange("s p b -> p s b").bitcast(I32),
+                    )
         load_scale_rows(w2_plane, w2_scales)
         nc.sync.dma_start(
             out=w2_sb[:].bitcast(I32).rearrange("p (e b) -> p e b", e=E),
@@ -108,16 +110,19 @@ def tile_moe_ecr_glu_gelu_kernel(
         for r, pos in enumerate((pos1, pos2, pos3)):
             pos_sb.append(lists.tile([P, T // LIST], U16, name=f"pos_sb{r}"))
             nc.sync.dma_start(pos_sb[r][:], pos)
-        gate_sb = [held(f"gate{r}", [P, T], F32) for r in range(TOP)]
-        for r in range(TOP):
-            nc.sync.dma_start(out=gate_sb[r][:], in_=gate[r])
+        gate_sb = {}
+        for t0, width in ((0, HEAD), (HEAD, T - HEAD)):
+            gate_sb[t0] = held(f"gate{t0}", [P, TOP * width], F32)
+            nc.sync.dma_start(
+                out=gate_sb[t0][:].rearrange("n (r t) -> n r t", r=TOP),
+                in_=gate[:, :, t0:t0 + width].rearrange("r n t -> n r t"),
+            )
 
         slot_codes, slot_planes = {}, {}
 
         def quantise_tokens(s):
             for t0, width, engine in CASTS[s]:
-                l0 = max(first for first, count in LOADS[s] if first <= t0)
-                src = raw[s, l0][:, :, t0 - l0:t0 - l0 + width].rearrange("p j (c i) -> p c j i", i=4)
+                src = raw[s][:, :, t0:t0 + width].rearrange("p j (c i) -> p c j i", i=4)
                 grouped = held(f"grouped{s}_{t0}", [P, width * PACK], BF16)
                 dst = grouped[:].rearrange("p (c i j) -> p c j i", i=4, j=PACK)
                 if engine == "vector":
@@ -130,36 +135,36 @@ def tile_moe_ecr_glu_gelu_kernel(
                     in_=grouped[:],
                 )
 
-        def gather_tokens(s, pair):
-            part = offs_sb[:, pair * PAIR * C // LIST:(pair + 1) * PAIR * C // LIST]
-            slot_codes[s, pair] = ring.tile([P, PAIR * C], U32, name=f"slot_codes{s}", align_bytes=64)
-            slot_planes[s, pair] = ring.tile([P, PAIR * C], U8, name=f"slot_plane{s}", align_bytes=64)
-            nc.vector.tensor_copy(slot_codes[s, pair][:], x_codes[s][:].indirect(part))
-            nc.vector.tensor_copy(slot_planes[s, pair][:], x_planes[s][:].indirect(part))
+        def gather_tokens(s, e):
+            part = offs_sb[:, e * C // LIST:(e + 1) * C // LIST]
+            slot_codes[s, e] = ring.tile([P, C], U32, name=f"slot_codes{s}", align_bytes=64)
+            slot_planes[s, e] = ring.tile([P, C], U8, name=f"slot_plane{s}", align_bytes=64)
+            nc.vector.tensor_copy(slot_codes[s, e][:], x_codes[s][:].indirect(part))
+            nc.vector.tensor_copy(slot_planes[s, e][:], x_planes[s][:].indirect(part))
 
         for s in range(PASSES):
             quantise_tokens(s)
-            for pair in range(PAIRS_HELD):
-                gather_tokens(s, pair)
+            for e in range(AHEAD):
+                gather_tokens(s, e)
 
-        hidden, h_codes, h_plane = {}, {}, {}
+        hidden, h_codes, h_plane, gelu_bank = {}, {}, {}, {}
 
         def first_layer(e):
             sums = []
             for m in range(2):
-                acc = psum.tile([P, H], F32, name=f"acc{m}", bufs=3)
+                acc = psum.tile([P, H], F32, name=f"acc{m}", bufs=BANKS[m])
                 for s in range(PASSES):
-                    first = (e * PASSES + s) * H
-                    slots = slice((e % PAIR) * C, (e % PAIR + 1) * C)
                     nc.tensor.matmul_mx(
                         out=acc[:],
-                        lhsT=slot_codes[s, e // PAIR][:, slots].bitcast(FP8X4),
-                        lhsT_scale=slot_planes[s, e // PAIR][:, slots],
+                        lhsT=slot_codes[s, e][:].bitcast(FP8X4),
+                        lhsT_scale=slot_planes[s, e][:],
                         rhs=w_words[e, m][:, s * 2 * H:(s + 1) * 2 * H].bitcast(FP4X4),
-                        rhs_scale=w_planes[m][:, first:first + H],
+                        rhs_scale=w_plane[e, m][:, s * H:(s + 1) * H],
                         start=(s == 0),
                         stop=(s == PASSES - 1),
                     )
+                if m == 0:
+                    gelu_bank[e] = acc
                 sums.append(acc[:].rearrange("c (p u v) -> c u p v", u=2, v=2))
             act = work.tile([P, H], F32, name="act")
             act_view = act[:].rearrange("c (u p v) -> c u p v", u=2, v=2)
@@ -171,20 +176,24 @@ def tile_moe_ecr_glu_gelu_kernel(
 
         def turn_hidden(e):
             pairs = hidden[e][:].bitcast(F32)
-            turned = psum.tile([P, 2, C], F32, name="turned")
+            if e + LAG < E:
+                bank = gelu_bank[e + LAG]
+            else:
+                bank = psum.tile([P, 2 * C], F32, name="turned")
+            turned = bank[:, :2 * C].rearrange("p (u c) -> p u c", u=2)
             for u in range(2):
                 nc.tensor.transpose(turned[:, u, :], pairs[:, u * P:(u + 1) * P], ident[:])
             grouped_h = work.tile([P, C * PACK], BF16, name="grouped_h", align_bytes=64)
             nc.scalar.copy(
                 out=grouped_h[:].bitcast(F32).rearrange("p (c u) -> p c u", u=2),
-                in_=turned[:].rearrange("p u c -> p c u"),
+                in_=turned.rearrange("p u c -> p c u"),
             )
             h_codes[e] = held(f"h_codes{e}", [P, C], U32)
             h_plane[e] = held(f"h_plane{e}", [P, C], U8)
             nc.vector.quantize_mx(out=h_codes[e][:].bitcast(FP8X4), scales=h_plane[e][:], in_=grouped_h[:])
 
         def second_layer(experts):
-            y_acc = psum.tile([P, len(experts) * C], F32, name="acc1", bufs=3)
+            y_acc = psum.tile([P, len(experts) * C], F32, name="acc1", bufs=BANKS[1])
             for i, e in enumerate(experts):
                 nc.tensor.matmul_mx(
                     out=y_acc[:, i * C:(i + 1) * C],
@@ -200,23 +209,44 @@ def tile_moe_ecr_glu_gelu_kernel(
         for step in range(E + LAG):
             if step < E:
                 first_layer(step)
-            if step == PAIR - 1:
+            if step + AHEAD < E:
                 for s in range(PASSES):
-                    gather_tokens(s, PAIRS_HELD)
+                    gather_tokens(s, step + AHEAD)
             if step >= LAG:
                 turn_hidden(step - LAG)
         for experts in BANKS_OF_Y:
             second_layer(experts)
 
-        for t0, width in OUT_PARTS:
+        def gated_terms(t0, width):
             terms = []
             for r in range(TOP):
                 term = held(f"term{r}_{t0}", [P, width], F32)
                 part = pos_sb[r][:, t0 // LIST:(t0 + width) // LIST]
-                nc.vector.tensor_tensor(term[:], y[:].indirect(part), gate_sb[r][:, t0:t0 + width], MULT)
+                nc.vector.tensor_tensor(term[:], y[:].indirect(part), gate_sb[t0][:, r * width:(r + 1) * width], MULT)
                 terms.append(term)
-            partial = held(f"partial{t0}", [P, width], F32)
-            nc.vector.tensor_tensor(partial[:], terms[0][:], terms[1][:], ADD)
-            total = held(f"total{t0}", [P, width], F32)
-            nc.vector.tensor_tensor(total[:], partial[:], terms[2][:], ADD)
-            nc.sync.dma_start(out=out[:, t0:t0 + width], in_=total[:])
+            return terms
+
+        terms = gated_terms(0, HEAD)
+        blocks = HEAD // P
+        sums = [psum.tile([P, P], F32, name="acc0", bufs=BANKS[0]) for b in range(blocks)]
+        for r in range(TOP):
+            for b in range(blocks):
+                nc.tensor.matmul(
+                    sums[b][:], terms[r][:, b * P:(b + 1) * P], ident[:],
+                    start=(r == 0), stop=(r == TOP - 1), is_transpose=True,
+                )
+        back = psum.tile([P, HEAD], F32, name="acc1", bufs=BANKS[1])
+        for b in range(blocks):
+            by_token = held(f"by_token{b}", [P, P], F32)
+            nc.scalar.copy(out=by_token[:], in_=sums[b][:])
+            nc.tensor.transpose(back[:, b * P:(b + 1) * P], by_token[:], ident[:])
+        head = held("head", [P, HEAD], F32)
+        nc.scalar.copy(out=head[:], in_=back[:])
+        nc.sync.dma_start(out=out[:, :HEAD], in_=head[:])
+
+        terms = gated_terms(HEAD, T - HEAD)
+        partial = held("partial", [P, T - HEAD], F32)
+        nc.vector.tensor_tensor(partial[:], terms[0][:], terms[1][:], ADD)
+        total = held("total", [P, T - HEAD], F32)
+        nc.vector.tensor_tensor(total[:], partial[:], terms[2][:], ADD)
+        nc.sync.dma_start(out=out[:, HEAD:], in_=total[:])

from contextlib import ExitStack

import concourse.mybir as mybir
from concourse.masks import make_identity

K, T, E, C, H, N = 1024, 640, 6, 128, 512, 128
TOP = 3
PAD = 64
SLOTS = E * C
FLOPS = 2 * SLOTS * (2 * K * H + H * N)

F32 = mybir.dt.float32
BF16 = mybir.dt.bfloat16
I32 = mybir.dt.int32
U32 = mybir.dt.uint32
U16 = mybir.dt.uint16
U8 = mybir.dt.uint8
FP8X4 = mybir.dt.float8_e4m3fn_x4
FP4X4 = mybir.dt.float4_e2m1fn_x4
ACT = mybir.ActivationFunctionType
MULT = mybir.AluOpType.mult
ADD = mybir.AluOpType.add

P = 128
PACK = 4
K_PASS = P * PACK
PASSES = K // K_PASS
LIST = 16
AHEAD = 3

CASTS = (
    ((0, 256, "vector"), (256, 256, "scalar"), (512, 128, "vector")),
    ((0, 256, "scalar"), (256, 256, "scalar"), (512, 128, "vector")),
)
SCALE_GROUPS = ((0, 1, 2), (3, 4, 5))
LAG = 2
BANKS_OF_Y = ((0, 1, 2, 3), (4,), (5,))
HEAD = 256
BANKS = (2, 4)


def tile_moe_ecr_glu_gelu_kernel(
    tc, xT, w1_words, w1_scales, w3_words, w3_scales, w2_words, w2_scales, gate, offs, pos1, pos2, pos3, out
):
    nc = tc.nc

    with ExitStack() as ctx:
        lists = ctx.enter_context(tc.tile_pool(name="lists", bufs=1))
        keep = ctx.enter_context(tc.tile_pool(name="keep", bufs=1))
        work = ctx.enter_context(tc.tile_pool(name="work", bufs=4))
        ring = ctx.enter_context(tc.tile_pool(name="ring", bufs=AHEAD))
        psum = ctx.enter_context(tc.psum_pool(name="psum", bufs=2))

        def held(name, shape, dtype):
            return keep.tile(shape, dtype, name=name, align_bytes=64)

        def load_scale_rows(plane, scales):
            rows = scales.rearrange("e s (q r) n -> r q (e s) n", r=4).bitcast(I32)
            words = plane[:].bitcast(I32).rearrange("p (a n) -> p a n", n=rows.shape[3])
            for r in range(4):
                nc.sync.dma_start(out=words[r:P:32], in_=rows[r])

        w_planes = [
            [held(f"w{m}_plane{g}", [P, len(experts) * PASSES * H], U8) for m in range(2)]
            for g, experts in enumerate(SCALE_GROUPS)
        ]
        w2_plane = held("w2_plane", [P, E * N], U8)
        for plane in w_planes[0] + w_planes[1] + [w2_plane]:
            nc.vector.memset(plane[:].bitcast(I32), 0)
        x_planes = [held(f"x_plane{s}", [P, T], U8) for s in range(PASSES)]
        x_codes = [held(f"x_codes{s}", [P, T], U32) for s in range(PASSES)]
        zeros = held("zeros", [P, PAD], F32)
        nc.gpsimd.memset(zeros[:], 0.0)
        for plane in x_planes:
            nc.gpsimd.memset(plane[:].bitcast(I32), 0)
        ident = held("ident", [P, P], F32)
        make_identity(nc, ident[:])
        y = held("y", [P, SLOTS + PAD], F32)
        nc.scalar.activation(out=y[:, SLOTS:], in_=zeros[:], func=ACT.Gelu_apprx_tanh)

        offs_sb = lists.tile([P, SLOTS // LIST], U16, name="offs_sb")
        raw = {}
        for s in range(PASSES):
            rows = xT[s * K_PASS:(s + 1) * K_PASS, :].rearrange("(p j) t -> p j t", j=PACK)
            raw[s] = held(f"raw{s}", [P, PACK, T], F32)
            nc.sync.dma_start(out=raw[s][:], in_=rows)
            if s == 0:
                nc.sync.dma_start(offs_sb[:], offs)

        w_words = {}
        w2_sb = held("w2_sb", [P, E * 2 * N], U8)
        w_plane = {}
        for g, experts in enumerate(SCALE_GROUPS):
            for m, scales in enumerate((w1_scales, w3_scales)):
                load_scale_rows(w_planes[g][m], scales[experts[0]:experts[-1] + 1])
            for i, e in enumerate(experts):
                for m, words in enumerate((w1_words, w3_words)):
                    w_plane[e, m] = w_planes[g][m][:, i * PASSES * H:(i + 1) * PASSES * H]
                    w_words[e, m] = held(f"w{m}_words{e}", [P, PASSES * 2 * H], U8)
                    nc.sync.dma_start(
                        out=w_words[e, m][:].bitcast(I32).rearrange("p (s b) -> p s b", s=PASSES),
                        in_=words[e].rearrange("s p b -> p s b").bitcast(I32),
                    )
        load_scale_rows(w2_plane, w2_scales)
        nc.sync.dma_start(
            out=w2_sb[:].bitcast(I32).rearrange("p (e b) -> p e b", e=E),
            in_=w2_words.rearrange("e s p b -> p (e s) b").bitcast(I32),
        )
        pos_sb = []
        for r, pos in enumerate((pos1, pos2, pos3)):
            pos_sb.append(lists.tile([P, T // LIST], U16, name=f"pos_sb{r}"))
            nc.sync.dma_start(pos_sb[r][:], pos)
        gate_sb = {}
        for t0, width in ((0, HEAD), (HEAD, T - HEAD)):
            gate_sb[t0] = held(f"gate{t0}", [P, TOP * width], F32)
            nc.sync.dma_start(
                out=gate_sb[t0][:].rearrange("n (r t) -> n r t", r=TOP),
                in_=gate[:, :, t0:t0 + width].rearrange("r n t -> n r t"),
            )

        slot_codes, slot_planes = {}, {}

        def quantise_tokens(s):
            for t0, width, engine in CASTS[s]:
                src = raw[s][:, :, t0:t0 + width].rearrange("p j (c i) -> p c j i", i=4)
                grouped = held(f"grouped{s}_{t0}", [P, width * PACK], BF16)
                dst = grouped[:].rearrange("p (c i j) -> p c j i", i=4, j=PACK)
                if engine == "vector":
                    nc.vector.tensor_copy(out=dst, in_=src)
                else:
                    nc.scalar.activation(out=dst, in_=src, func=ACT.Copy)
                nc.vector.quantize_mx(
                    out=x_codes[s][:, t0:t0 + width].bitcast(FP8X4),
                    scales=x_planes[s][:, t0:t0 + width],
                    in_=grouped[:],
                )

        def gather_tokens(s, e):
            part = offs_sb[:, e * C // LIST:(e + 1) * C // LIST]
            slot_codes[s, e] = ring.tile([P, C], U32, name=f"slot_codes{s}", align_bytes=64)
            slot_planes[s, e] = ring.tile([P, C], U8, name=f"slot_plane{s}", align_bytes=64)
            nc.vector.tensor_copy(slot_codes[s, e][:], x_codes[s][:].indirect(part))
            nc.vector.tensor_copy(slot_planes[s, e][:], x_planes[s][:].indirect(part))

        for s in range(PASSES):
            quantise_tokens(s)
            for e in range(AHEAD):
                gather_tokens(s, e)

        hidden, h_codes, h_plane, gelu_bank = {}, {}, {}, {}

        def first_layer(e):
            sums = []
            for m in range(2):
                acc = psum.tile([P, H], F32, name=f"acc{m}", bufs=BANKS[m])
                for s in range(PASSES):
                    nc.tensor.matmul_mx(
                        out=acc[:],
                        lhsT=slot_codes[s, e][:].bitcast(FP8X4),
                        lhsT_scale=slot_planes[s, e][:],
                        rhs=w_words[e, m][:, s * 2 * H:(s + 1) * 2 * H].bitcast(FP4X4),
                        rhs_scale=w_plane[e, m][:, s * H:(s + 1) * H],
                        start=(s == 0),
                        stop=(s == PASSES - 1),
                    )
                if m == 0:
                    gelu_bank[e] = acc
                sums.append(acc[:].rearrange("c (p u v) -> c u p v", u=2, v=2))
            act = work.tile([P, H], F32, name="act")
            act_view = act[:].rearrange("c (u p v) -> c u p v", u=2, v=2)
            nc.scalar.activation(out=act_view, in_=sums[0], func=ACT.Gelu_apprx_tanh)
            hidden[e] = work.tile([P, H], BF16, name="hidden")
            nc.vector.tensor_tensor(
                hidden[e][:].rearrange("c (u p v) -> c u p v", u=2, v=2), sums[1], act_view, MULT
            )

        def turn_hidden(e):
            pairs = hidden[e][:].bitcast(F32)
            if e + LAG < E:
                bank = gelu_bank[e + LAG]
            else:
                bank = psum.tile([P, 2 * C], F32, name="turned")
            turned = bank[:, :2 * C].rearrange("p (u c) -> p u c", u=2)
            for u in range(2):
                nc.tensor.transpose(turned[:, u, :], pairs[:, u * P:(u + 1) * P], ident[:])
            grouped_h = work.tile([P, C * PACK], BF16, name="grouped_h", align_bytes=64)
            nc.scalar.copy(
                out=grouped_h[:].bitcast(F32).rearrange("p (c u) -> p c u", u=2),
                in_=turned.rearrange("p u c -> p c u"),
            )
            h_codes[e] = held(f"h_codes{e}", [P, C], U32)
            h_plane[e] = held(f"h_plane{e}", [P, C], U8)
            nc.vector.quantize_mx(out=h_codes[e][:].bitcast(FP8X4), scales=h_plane[e][:], in_=grouped_h[:])

        def second_layer(experts):
            y_acc = psum.tile([P, len(experts) * C], F32, name="acc1", bufs=BANKS[1])
            for i, e in enumerate(experts):
                nc.tensor.matmul_mx(
                    out=y_acc[:, i * C:(i + 1) * C],
                    lhsT=w2_sb[:, e * 2 * N:(e + 1) * 2 * N].bitcast(FP4X4),
                    lhsT_scale=w2_plane[:, e * N:(e + 1) * N],
                    rhs=h_codes[e][:].bitcast(FP8X4),
                    rhs_scale=h_plane[e][:],
                    start=True,
                    stop=True,
                )
            nc.scalar.copy(out=y[:, experts[0] * C:(experts[-1] + 1) * C], in_=y_acc[:])

        for step in range(E + LAG):
            if step < E:
                first_layer(step)
            if step + AHEAD < E:
                for s in range(PASSES):
                    gather_tokens(s, step + AHEAD)
            if step >= LAG:
                turn_hidden(step - LAG)
        for experts in BANKS_OF_Y:
            second_layer(experts)

        def gated_terms(t0, width):
            terms = []
            for r in range(TOP):
                term = held(f"term{r}_{t0}", [P, width], F32)
                part = pos_sb[r][:, t0 // LIST:(t0 + width) // LIST]
                nc.vector.tensor_tensor(term[:], y[:].indirect(part), gate_sb[t0][:, r * width:(r + 1) * width], MULT)
                terms.append(term)
            return terms

        terms = gated_terms(0, HEAD)
        blocks = HEAD // P
        sums = [psum.tile([P, P], F32, name="acc0", bufs=BANKS[0]) for b in range(blocks)]
        for r in range(TOP):
            for b in range(blocks):
                nc.tensor.matmul(
                    sums[b][:], terms[r][:, b * P:(b + 1) * P], ident[:],
                    start=(r == 0), stop=(r == TOP - 1), is_transpose=True,
                )
        back = psum.tile([P, HEAD], F32, name="acc1", bufs=BANKS[1])
        for b in range(blocks):
            by_token = held(f"by_token{b}", [P, P], F32)
            nc.scalar.copy(out=by_token[:], in_=sums[b][:])
            nc.tensor.transpose(back[:, b * P:(b + 1) * P], by_token[:], ident[:])
        head = held("head", [P, HEAD], F32)
        nc.scalar.copy(out=head[:], in_=back[:])
        nc.sync.dma_start(out=out[:, :HEAD], in_=head[:])

        terms = gated_terms(HEAD, T - HEAD)
        partial = held("partial", [P, T - HEAD], F32)
        nc.vector.tensor_tensor(partial[:], terms[0][:], terms[1][:], ADD)
        total = held("total", [P, T - HEAD], F32)
        nc.vector.tensor_tensor(total[:], partial[:], terms[2][:], ADD)
        nc.sync.dma_start(out=out[:, HEAD:], in_=total[:])
